import numpy as np
import ml_dtypes


def mxq(x, axis, fmt="e4m3"):
    dtype, down = {"e4m3": (ml_dtypes.float8_e4m3fn, 7), "e5m2": (ml_dtypes.float8_e5m2, 14)}[fmt]
    v = np.moveaxis(np.asarray(x, np.float32).astype(ml_dtypes.bfloat16).astype(np.float64), axis, -1)
    blocks = v.reshape(v.shape[:-1] + (-1, 32))
    amax = np.abs(blocks).max(-1, keepdims=True)
    byte = np.maximum(np.where(amax > 0, np.frexp(amax)[1] - 1 + 127, 0) - down, 1)
    scale = np.exp2(byte - 127.0)
    codes = (blocks / scale).astype(np.float32).astype(dtype).astype(np.float64)
    return np.moveaxis((codes * scale).reshape(v.shape), -1, axis)


WIDE = False


def mx_kscale(k):
    if not WIDE:
        return np.ones(k)
    levels = np.array([10, -10, 5, -5, 0])
    if k % 512:
        return np.exp2(np.random.permutation(np.resize(levels, k // 32))).repeat(32)
    a = np.empty((k // 512, 16))
    for p in range(k // 512):
        a[p, :8] = np.random.permutation(np.resize(levels, 8))
        for g in range(8):
            far = levels[np.abs(levels - a[p, g]) >= 10]
            a[p, g + 8] = far[np.random.randint(len(far))]
    return np.exp2(a.ravel()).repeat(32)


def f64(x):
    return np.asarray(x).astype(np.float64)


def striped(idx):
    return np.tile(idx.reshape(-1, 16).T, (8, 1)).astype(np.uint16)


def unstriped(offs):
    return offs[:16].T.reshape(-1).astype(np.int64)


def pack_weight(w):
    k, n = w.shape
    w = f64(np.asarray(w, np.float32).astype(ml_dtypes.bfloat16)).reshape(k // 32, 32, n)
    amax = np.abs(w).max(1)
    byte = np.clip(np.where(amax > 0, np.frexp(amax)[1] - 1 + 127 - 7, 1), 1, 254)
    scaled = (w * np.exp2(127.0 - byte)[:, None, :]).reshape(k, n).astype(np.float32)
    words = np.ascontiguousarray(scaled.reshape(k // 512, 128, 4, n).transpose(0, 1, 3, 2)).astype(ml_dtypes.float8_e4m3fn).view(np.uint8)
    return words, np.ascontiguousarray(byte.astype(np.uint8).reshape(k // 512, 16, n))


def unpack_weight(words, scales):
    g, p, n, _ = words.shape
    vals = np.ascontiguousarray(words).view(ml_dtypes.float8_e4m3fn).astype(np.float64) * np.repeat(np.exp2(scales.astype(np.float64) - 127.0), 8, axis=1)[..., None]
    return vals.transpose(0, 1, 3, 2).reshape(g * 512, n)


def relu(v):
    return np.maximum(v, 0.0)


K, T, D, S, V, N = 1024, 2048, 4, 2048, 512, 256


def setup_inputs():
    n = np.random.standard_normal
    s = mx_kscale(K)[:, None]
    words, scales = pack_weight(n((K, N)) / np.sqrt(K) / s)
    return {
        "xT": (n((K, T)) * s / np.sqrt(D)).astype(ml_dtypes.bfloat16).astype(np.float32),
        "w_words": words,
        "w_scales": scales,
        "b": (0.3 * n((N, 1))).astype(np.float32),
        "offs": striped(np.concatenate([np.random.permutation(T)[:V] for _ in range(D)])),
    }


def reference(xT, w_words, w_scales, b, offs):
    w = unpack_weight(w_words, w_scales)
    idx = unstriped(offs)
    x = sum(f64(xT)[:, idx[d * V:(d + 1) * V]] for d in range(D))
    return relu((w.T @ mxq(x, 0, "e4m3")) + f64(b))

@@ -1,0 +1,180 @@
+from contextlib import ExitStack
+
+import concourse.mybir as mybir
+from concourse.masks import make_identity
+
+K, T, D, V, N = 1024, 2048, 4, 512, 256
+FLOPS = 2 * K * V * N
+
+F32 = mybir.dt.float32
+BF16 = mybir.dt.bfloat16
+I32 = mybir.dt.int32
+U32 = mybir.dt.uint32
+U16 = mybir.dt.uint16
+U8 = mybir.dt.uint8
+FP8X4 = mybir.dt.float8_e4m3fn_x4
+ACT = mybir.ActivationFunctionType
+ALU = mybir.AluOpType
+
+P = 128
+HALF = V // 2
+PLANES = 8
+SCALAR_PIECES = [2, 2, 0, 4, 0, 3, 0, 2]
+LOAD_CHUNKS = [4, 4, 1, 2, 1, 2, 1, 2]
+SLOTS = 6
+
+
+def tile_picked_hash_lin_relu_sub_l_kernel(tc, xT, w_words, w_scales, b, offs, out):
+    nc = tc.nc
+    with ExitStack() as ctx:
+        keep = ctx.enter_context(tc.tile_pool(name="keep", bufs=1))
+        psum = ctx.enter_context(tc.psum_pool(name="psum", bufs=1))
+
+        offsets = keep.tile([P, T // 16], U16, name="offsets")
+        nc.sync.dma_start(offsets[:], offs)
+
+        rows = xT.rearrange("(a p t) n -> a t p n", a=2, t=4)
+        raw = [keep.tile([P, T], F32, name=f"raw{j}") for j in range(PLANES)]
+        for j in range(PLANES):
+            width = T // LOAD_CHUNKS[j]
+            for c in range(LOAD_CHUNKS[j]):
+                cols = slice(c * width, (c + 1) * width)
+                nc.sync.dma_start(out=raw[j][:, cols], in_=rows[j // 4, j % 4][:, cols])
+
+        w_codes = keep.tile([P, 2, N], U32, name="w_codes", align_bytes=64)
+        w_plane = keep.tile([P, 2, N], U8, name="w_plane", align_bytes=64)
+        nc.vector.memset(w_plane[:].rearrange("p a n -> p (a n)").bitcast(U32), 0)
+        for q in range(4):
+            nc.sync.dma_start(
+                out=w_plane[32 * q : 32 * q + 4, :, :].bitcast(I32),
+                in_=w_scales[:, 4 * q : 4 * q + 4, :].rearrange("a r n -> r a n").bitcast(I32),
+            )
+        nc.sync.dma_start(
+            out=w_codes[:].bitcast(I32),
+            in_=w_words.rearrange("a p n r -> p a (n r)").bitcast(I32),
+        )
+        bias = [keep.tile([P, 1], F32, name=f"bias{m}") for m in range(2)]
+        for m in range(2):
+            nc.sync.dma_start(out=bias[m][:], in_=b[m * P : (m + 1) * P, :])
+
+        ident = keep.tile([P, P], F32, name="ident")
+        make_identity(nc, ident[:])
+
+        slots = [keep.tile([P, V], F32, name=f"slot{s}") for s in range(SLOTS)]
+        for s in range(SLOTS):
+            nc.vector.memset(slots[s][:], 0.0)
+        warm = keep.tile([P, 1], F32, name="warm")
+        nc.scalar.activation(out=warm[:], in_=slots[0][:, 0:1], func=ACT.Relu)
+
+        narrow = {}
+        for j in range(PLANES):
+            if SCALAR_PIECES[j]:
+                narrow[j] = keep.tile([P, T], BF16, name=f"narrow{j}")
+                width = T // LOAD_CHUNKS[j]
+                for c in range(LOAD_CHUNKS[j]):
+                    cols = slice(c * width, (c + 1) * width)
+                    nc.gpsimd.tensor_scalar(narrow[j][:, cols], raw[j][:, cols], 1.0, 0.0, ALU.mult, ALU.add)
+
+        picked = {}
+        used_slots = []
+
+        def gather(j, d, lo, hi):
+            part = offsets[:, (d * V + lo) // 16 : (d * V + hi) // 16]
+            if d >= D - SCALAR_PIECES[j]:
+                if (j, d) not in picked:
+                    picked[(j, d)] = slots[len(used_slots) % SLOTS]
+                    used_slots.append(j)
+                upper = picked[(j, d)][:].bitcast(BF16).rearrange("p (v h) -> p v h", h=2)
+                nc.scalar.activation(out=upper[:, lo:hi, 1], in_=narrow[j][:].indirect(part), func=ACT.Copy)
+            else:
+                if (j, d) not in picked:
+                    picked[(j, d)] = keep.tile([P, V], F32, name=f"picked{j}_{d}")
+                nc.vector.tensor_copy(out=picked[(j, d)][:, lo:hi], in_=raw[j][:].indirect(part))
+
+        sums = {}
+        count = {}
+
+        def add_up(j, d, h):
+            pair, e = j // 2, j % 2
+            if (pair, h) not in sums:
+                sums[(pair, h)] = psum.tile([P, 2, 2, P], F32, name=f"sums{pair}_{h}", tag=f"sums{pair % 2}_{h}")
+                count[(pair, h)] = 0
+            for vb in range(2):
+                lo = h * HALF + vb * P
+                nc.tensor.matmul(
+                    sums[(pair, h)][:, vb, e, :],
+                    lhsT=picked[(j, d)][:, lo : lo + P],
+                    rhs=ident[:],
+                    start=(count[(pair, h)] == 0),
+                    stop=(count[(pair, h)] == 4 * D - 1),
+                    is_transpose=True,
+                )
+                count[(pair, h)] += 1
+
+        back = {}
+
+        def round_and_turn(pair, h):
+            a, u = pair // 2, pair % 2
+            rounded = keep.tile([P, 2, P, 2], BF16, name=f"rounded{pair}_{h}")
+            nc.scalar.copy(out=rounded[:], in_=sums[(pair, h)][:].rearrange("v b e p -> v b p e"))
+            words = rounded[:].rearrange("v b p e -> v (b p e)").bitcast(F32)
+            if (a, h) not in back:
+                back[(a, h)] = psum.tile([P, 2, HALF], F32, name=f"back{a}_{h}", tag=f"back{h}")
+            for vb in range(2):
+                nc.tensor.transpose(back[(a, h)][:, u, vb * P : (vb + 1) * P], words[:, vb * P : (vb + 1) * P], ident[:])
+
+        acc = {}
+
+        def quantise_and_multiply(a, h, engine):
+            grouped = keep.tile([P, HALF * 4], BF16, name=f"grouped{a}_{h}", align_bytes=64)
+            dst = grouped[:].bitcast(F32).rearrange("p (v u) -> p v u", u=2)
+            src = back[(a, h)][:].rearrange("p u v -> p v u")
+            if engine == "scalar":
+                nc.scalar.copy(out=dst, in_=src)
+            else:
+                nc.vector.tensor_copy(out=dst, in_=src)
+            codes = keep.tile([P, HALF], U32, name=f"codes{a}_{h}", align_bytes=64)
+            plane = keep.tile([P, HALF], U8, name=f"plane{a}_{h}", align_bytes=64)
+            nc.vector.quantize_mx(out=codes[:].bitcast(FP8X4), scales=plane[:], in_=grouped[:])
+            for m in range(2):
+                if a == 0:
+                    tag = f"acc{m}" if h == 0 else f"sums0_{m}"
+                    acc[(m, h)] = psum.tile([P, HALF], F32, name=f"acc{m}_{h}", tag=tag)
+                nc.tensor.matmul_mx(
+                    out=acc[(m, h)][:],
+                    lhsT=w_codes[:, a, m * P : (m + 1) * P].bitcast(FP8X4),
+                    lhsT_scale=w_plane[:, a, m * P : (m + 1) * P],
+                    rhs=codes[:].bitcast(FP8X4),
+                    rhs_scale=plane[:],
+                    start=(a == 0),
+                    stop=(a == 1),
+                )
+
+        def finish(h):
+            for m in range(2):
+                result = keep.tile([P, HALF], F32, name=f"result{m}_{h}")
+                if m == 0:
+                    nc.scalar.activation(out=result[:], in_=acc[(m, h)][:], func=ACT.Relu, bias=bias[m][:])
+                else:
+                    nc.vector.tensor_scalar(result[:], acc[(m, h)][:], bias[m][:], 0.0, ALU.add, ALU.max)
+                nc.sync.dma_start(out=out[m * P : (m + 1) * P, h * HALF : (h + 1) * HALF], in_=result[:])
+
+        for pair in range(3):
+            for j in (2 * pair, 2 * pair + 1):
+                for d in range(D):
+                    gather(j, d, 0, V)
+                    for h in range(2):
+                        add_up(j, d, h)
+            for h in range(2):
+                round_and_turn(pair, h)
+            if pair == 1:
+                quantise_and_multiply(0, 0, "scalar")
+        quantise_and_multiply(0, 1, "scalar")
+        for h in range(2):
+            for j in (6, 7):
+                for d in range(D):
+                    gather(j, d, h * HALF, (h + 1) * HALF)
+                    add_up(j, d, h)
+            round_and_turn(3, h)
+            quantise_and_multiply(1, h, "vector" if h == 1 else "scalar")
+            finish(h)

@@ -18,10 +18,8 @@ ALU = mybir.AluOpType
 
 P = 128
 HALF = V // 2
-PLANES = 8
-SCALAR_PIECES = [2, 2, 0, 4, 0, 3, 0, 2]
-LOAD_CHUNKS = [4, 4, 1, 2, 1, 2, 1, 2]
-SLOTS = 6
+CHUNK = 512
+PACKERS = {1: "GVVV", 2: "SSSS", 3: "SSSS"}
 
 
 def tile_picked_hash_lin_relu_sub_l_kernel(tc, xT, w_words, w_scales, b, offs, out):
@@ -33,13 +31,17 @@ def tile_picked_hash_lin_relu_sub_l_kernel(tc, xT, w_words, w_scales, b, offs, o
         offsets = keep.tile([P, T // 16], U16, name="offsets")
         nc.sync.dma_start(offsets[:], offs)
 
-        rows = xT.rearrange("(a p t) n -> a t p n", a=2, t=4)
-        raw = [keep.tile([P, T], F32, name=f"raw{j}") for j in range(PLANES)]
-        for j in range(PLANES):
-            width = T // LOAD_CHUNKS[j]
-            for c in range(LOAD_CHUNKS[j]):
-                cols = slice(c * width, (c + 1) * width)
-                nc.sync.dma_start(out=raw[j][:, cols], in_=rows[j // 4, j % 4][:, cols])
+        rows = xT.rearrange("(a p u e) n -> a u p e n", a=2, u=2, e=2)
+        chunks = [slice(c, c + CHUNK) for c in range(0, T, CHUNK)]
+        plane = [keep.tile([P, T], F32, name=f"plane{e}") for e in range(2)]
+        for e in range(2):
+            for cols in chunks:
+                nc.sync.dma_start(out=plane[e][:, cols], in_=rows[0, 0][:, e, cols])
+        raw = {}
+        for pair in (1, 2, 3):
+            for c, cols in enumerate(chunks):
+                raw[(pair, c)] = keep.tile([P, 2, CHUNK], F32, name=f"raw{pair}_{c}", tag=f"raw{pair}_{c}")
+                nc.sync.dma_start(out=raw[(pair, c)][:], in_=rows[pair // 2, pair % 2][:, :, cols])
 
         w_codes = keep.tile([P, 2, N], U32, name="w_codes", align_bytes=64)
         w_plane = keep.tile([P, 2, N], U8, name="w_plane", align_bytes=64)
@@ -60,121 +62,208 @@ def tile_picked_hash_lin_relu_sub_l_kernel(tc, xT, w_words, w_scales, b, offs, o
         ident = keep.tile([P, P], F32, name="ident")
         make_identity(nc, ident[:])
 
-        slots = [keep.tile([P, V], F32, name=f"slot{s}") for s in range(SLOTS)]
-        for s in range(SLOTS):
-            nc.vector.memset(slots[s][:], 0.0)
+        widened = keep.tile([P, 4, V], F32, name="widened")
+        nc.vector.memset(widened[:].rearrange("p s v -> p (s v)"), 0.0)
         warm = keep.tile([P, 1], F32, name="warm")
-        nc.scalar.activation(out=warm[:], in_=slots[0][:, 0:1], func=ACT.Relu)
+        nc.scalar.activation(out=warm[:], in_=widened[:, 0, 0:1], func=ACT.Relu)
 
-        narrow = {}
-        for j in range(PLANES):
-            if SCALAR_PIECES[j]:
-                narrow[j] = keep.tile([P, T], BF16, name=f"narrow{j}")
-                width = T // LOAD_CHUNKS[j]
-                for c in range(LOAD_CHUNKS[j]):
-                    cols = slice(c * width, (c + 1) * width)
-                    nc.gpsimd.tensor_scalar(narrow[j][:, cols], raw[j][:, cols], 1.0, 0.0, ALU.mult, ALU.add)
+        narrow = [keep.tile([P, T], BF16, name=f"narrow{e}", tag=f"narrow{e}") for e in range(2)]
+        for cols in chunks:
+            nc.vector.tensor_copy(out=narrow[0][:, cols], in_=plane[0][:, cols])
+        for cols in chunks:
+            nc.gpsimd.tensor_scalar(narrow[1][:, cols], plane[1][:, cols], 1.0, 0.0, ALU.mult, ALU.add)
 
-        picked = {}
-        used_slots = []
-
-        def gather(j, d, lo, hi):
-            part = offsets[:, (d * V + lo) // 16 : (d * V + hi) // 16]
-            if d >= D - SCALAR_PIECES[j]:
-                if (j, d) not in picked:
-                    picked[(j, d)] = slots[len(used_slots) % SLOTS]
-                    used_slots.append(j)
-                upper = picked[(j, d)][:].bitcast(BF16).rearrange("p (v h) -> p v h", h=2)
-                nc.scalar.activation(out=upper[:, lo:hi, 1], in_=narrow[j][:].indirect(part), func=ACT.Copy)
-            else:
-                if (j, d) not in picked:
-                    picked[(j, d)] = keep.tile([P, V], F32, name=f"picked{j}_{d}")
-                nc.vector.tensor_copy(out=picked[(j, d)][:, lo:hi], in_=raw[j][:].indirect(part))
+        def piece(d, lo, hi):
+            return offsets[:, (d * V + lo) // 16 : (d * V + hi) // 16]
 
         sums = {}
         count = {}
 
-        def add_up(j, d, h):
-            pair, e = j // 2, j % 2
+        def add_up(pair, h, e, src, total):
             if (pair, h) not in sums:
-                sums[(pair, h)] = psum.tile([P, 2, 2, P], F32, name=f"sums{pair}_{h}", tag=f"sums{pair % 2}_{h}")
+                sums[(pair, h)] = psum.tile([P, 2, 2, P], F32, name=f"sums{pair}_{h}", tag=f"sums{min(pair, 1)}_{h}")
                 count[(pair, h)] = 0
             for vb in range(2):
                 lo = h * HALF + vb * P
                 nc.tensor.matmul(
                     sums[(pair, h)][:, vb, e, :],
-                    lhsT=picked[(j, d)][:, lo : lo + P],
+                    lhsT=src[:, lo : lo + P],
                     rhs=ident[:],
                     start=(count[(pair, h)] == 0),
-                    stop=(count[(pair, h)] == 4 * D - 1),
+                    stop=(count[(pair, h)] == total - 1),
                     is_transpose=True,
                 )
                 count[(pair, h)] += 1
 
+        picked = {(e, d): keep.tile([P, V], F32, name=f"picked{e}_{d}") for e in range(2) for d in (0, 2)}
+
+        def first_pair(e, d, halves):
+            for lo, hi in halves:
+                if d % 2 == 0:
+                    dst = picked[(e, d)][:]
+                    nc.vector.tensor_copy(out=dst[:, lo:hi], in_=plane[e][:].indirect(piece(d, lo, hi)))
+                else:
+                    dst = widened[:, 2 * e + d // 2, :]
+                    upper = dst.bitcast(BF16).rearrange("p (v h) -> p v h", h=2)
+                    nc.scalar.activation(out=upper[:, lo:hi, 1], in_=narrow[e][:].indirect(piece(d, lo, hi)), func=ACT.Copy)
+                for h in range(lo // HALF, hi // HALF):
+                    add_up(0, h, e, dst, 4 * D)
+
+        packed = {}
+        last_chunk = len(chunks) - 1
+
+        def pack(pair):
+            tag = {1: "packed1", 2: "narrow1", 3: f"raw2_{last_chunk}"}[pair]
+            packed[pair] = keep.tile([P, T], U32, name=f"packed{pair}", tag=tag)
+            for c, (cols, who) in enumerate(zip(chunks, PACKERS[pair])):
+                dst = packed[pair][:, cols].bitcast(BF16).rearrange("p (n e) -> p n e", e=2)
+                src = raw[(pair, c)][:].rearrange("p e n -> p n e")
+                if who == "G":
+                    nc.gpsimd.tensor_scalar(dst, src, 1.0, 0.0, ALU.mult, ALU.add)
+                elif who == "V":
+                    nc.vector.tensor_copy(out=dst, in_=src)
+                else:
+                    nc.scalar.copy(out=dst, in_=src)
+
+        words = {pair: keep.tile([P, D * V], U32, name=f"words{pair}") for pair in (1, 2, 3)}
+
+        def looked_up(pair, d, lo, hi):
+            return words[pair][:, d * V + lo : d * V + hi]
+
+        def gather(pair, d, lo, hi):
+            nc.vector.tensor_copy(out=looked_up(pair, d, lo, hi), in_=packed[pair][:].indirect(piece(d, lo, hi)))
+
+        def middle_pair(pair):
+            for i in range(2):
+                gather(pair, 2 * i, 0, 2 * V)
+                two = keep.tile([P, 2, V], F32, name=f"two{pair}_{i}")
+                nc.gpsimd.tensor_tensor(
+                    two[:],
+                    looked_up(pair, 2 * i, 0, V).bitcast(BF16).rearrange("p (v e) -> p e v", e=2),
+                    looked_up(pair, 2 * i + 1, 0, V).bitcast(BF16).rearrange("p (v e) -> p e v", e=2),
+                    ALU.add,
+                )
+                for h in range(2):
+                    for e in range(2):
+                        add_up(pair, h, e, two[:, e, :], 8)
+
         back = {}
+        rounded = {}
 
         def round_and_turn(pair, h):
             a, u = pair // 2, pair % 2
-            rounded = keep.tile([P, 2, P, 2], BF16, name=f"rounded{pair}_{h}")
-            nc.scalar.copy(out=rounded[:], in_=sums[(pair, h)][:].rearrange("v b e p -> v b p e"))
-            words = rounded[:].rearrange("v b p e -> v (b p e)").bitcast(F32)
+            group = pair // 2
+            if group not in rounded:
+                tag = f"raw3_{last_chunk}" if group == 0 else "rounded_last"
+                rounded[group] = keep.tile([P, 2, 2, 2, P, 2], BF16, name=f"rounded{group}", tag=tag)
+            dst = rounded[group][:, u, h]
+            nc.scalar.copy(out=dst, in_=sums[(pair, h)][:].rearrange("v b e p -> v b p e"))
+            turned = dst.rearrange("v b p e -> v (b p e)").bitcast(F32)
             if (a, h) not in back:
                 back[(a, h)] = psum.tile([P, 2, HALF], F32, name=f"back{a}_{h}", tag=f"back{h}")
             for vb in range(2):
-                nc.tensor.transpose(back[(a, h)][:, u, vb * P : (vb + 1) * P], words[:, vb * P : (vb + 1) * P], ident[:])
+                nc.tensor.transpose(back[(a, h)][:, u, vb * P : (vb + 1) * P], turned[:, vb * P : (vb + 1) * P], ident[:])
+
+        grouped = {
+            (a, h): keep.tile([P, HALF * 4], BF16, name=f"grouped{a}_{h}", align_bytes=64) for a in range(2) for h in range(2)
+        }
+
+        def interleave(a, h):
+            dst = grouped[(a, h)][:].bitcast(F32).rearrange("p (v u) -> p v u", u=2)
+            if a == 0:
+                nc.scalar.copy(out=dst, in_=back[(a, h)][:].rearrange("p u v -> p v u"))
+            else:
+                nc.scalar.copy(out=dst[:, :, 0], in_=back[(a, h)][:, 0, :])
+
+        last_two = {}
+
+        def last_add(i, h, engine):
+            lo, hi = h * HALF, (h + 1) * HALF
+            last_two[(i, h)] = keep.tile([P, 2 * HALF], F32, name=f"last_two{i}_{h}")
+            engine.tensor_tensor(
+                last_two[(i, h)][:],
+                looked_up(3, 2 * i, lo, hi).bitcast(BF16),
+                looked_up(3, 2 * i + 1, lo, hi).bitcast(BF16),
+                ALU.add,
+            )
+
+        def last_sum(h):
+            nc.vector.tensor_tensor(
+                grouped[(1, h)][:].rearrange("p (v t) -> p v t", t=4)[:, :, 2:4],
+                last_two[(0, h)][:].rearrange("p (v e) -> p v e", e=2),
+                last_two[(1, h)][:].rearrange("p (v e) -> p v e", e=2),
+                ALU.add,
+            )
+
+        codes = {}
+        scales = {}
+
+        def quantise(a, h):
+            codes[(a, h)] = keep.tile([P, HALF], U32, name=f"codes{a}_{h}", align_bytes=64)
+            scales[(a, h)] = keep.tile([P, HALF], U8, name=f"scales{a}_{h}", align_bytes=64)
+            nc.vector.quantize_mx(out=codes[(a, h)][:].bitcast(FP8X4), scales=scales[(a, h)][:], in_=grouped[(a, h)][:])
 
         acc = {}
 
-        def quantise_and_multiply(a, h, engine):
-            grouped = keep.tile([P, HALF * 4], BF16, name=f"grouped{a}_{h}", align_bytes=64)
-            dst = grouped[:].bitcast(F32).rearrange("p (v u) -> p v u", u=2)
-            src = back[(a, h)][:].rearrange("p u v -> p v u")
-            if engine == "scalar":
-                nc.scalar.copy(out=dst, in_=src)
-            else:
-                nc.vector.tensor_copy(out=dst, in_=src)
-            codes = keep.tile([P, HALF], U32, name=f"codes{a}_{h}", align_bytes=64)
-            plane = keep.tile([P, HALF], U8, name=f"plane{a}_{h}", align_bytes=64)
-            nc.vector.quantize_mx(out=codes[:].bitcast(FP8X4), scales=plane[:], in_=grouped[:])
+        def multiply(a, h):
+            if a == 0 and h == 1:
+                both = psum.tile([P, 2, HALF], F32, name="acc_second", tag="back1")
+                acc[(0, 1)], acc[(1, 1)] = both[:, 0, :], both[:, 1, :]
+            if a == 0 and h == 0:
+                low = psum.tile([P, HALF], F32, name="acc_first0", tag="back0")
+                high = psum.tile([P, HALF], F32, name="acc_first1", tag="sums1_1")
+                acc[(0, 0)], acc[(1, 0)] = low[:], high[:]
             for m in range(2):
-                if a == 0:
-                    tag = f"acc{m}" if h == 0 else f"sums0_{m}"
-                    acc[(m, h)] = psum.tile([P, HALF], F32, name=f"acc{m}_{h}", tag=tag)
                 nc.tensor.matmul_mx(
-                    out=acc[(m, h)][:],
+                    out=acc[(m, h)],
                     lhsT=w_codes[:, a, m * P : (m + 1) * P].bitcast(FP8X4),
                     lhsT_scale=w_plane[:, a, m * P : (m + 1) * P],
-                    rhs=codes[:].bitcast(FP8X4),
-                    rhs_scale=plane[:],
-                    start=(a == 0),
-                    stop=(a == 1),
+                    rhs=codes[(a, h)][:].bitcast(FP8X4),
+                    rhs_scale=scales[(a, h)][:],
+                    start=(a == 0 and (h == 0 or m == 0)),
+                    stop=(a == 1 and (h == 0 or m == 1)),
                 )
 
         def finish(h):
             for m in range(2):
                 result = keep.tile([P, HALF], F32, name=f"result{m}_{h}")
-                if m == 0:
-                    nc.scalar.activation(out=result[:], in_=acc[(m, h)][:], func=ACT.Relu, bias=bias[m][:])
+                if m == 0 or h == 1:
+                    nc.scalar.activation(out=result[:], in_=acc[(m, h)], func=ACT.Relu, bias=bias[m][:])
                 else:
-                    nc.vector.tensor_scalar(result[:], acc[(m, h)][:], bias[m][:], 0.0, ALU.add, ALU.max)
+                    nc.vector.tensor_scalar(result[:], acc[(m, h)], bias[m][:], 0.0, ALU.add, ALU.max)
                 nc.sync.dma_start(out=out[m * P : (m + 1) * P, h * HALF : (h + 1) * HALF], in_=result[:])
 
-        for pair in range(3):
-            for j in (2 * pair, 2 * pair + 1):
-                for d in range(D):
-                    gather(j, d, 0, V)
-                    for h in range(2):
-                        add_up(j, d, h)
+        whole = [(0, V)]
+        halves = [(0, HALF), (HALF, V)]
+        for e in range(2):
+            for d in range(D):
+                first_pair(e, d, halves if (e, d) == (1, D - 1) else whole)
+        for pair in (1, 2, 3):
+            pack(pair)
+        for h in range(2):
+            round_and_turn(0, h)
+        for pair in (1, 2):
+            middle_pair(pair)
             for h in range(2):
                 round_and_turn(pair, h)
-            if pair == 1:
-                quantise_and_multiply(0, 0, "scalar")
-        quantise_and_multiply(0, 1, "scalar")
+            for h in range(2):
+                interleave(pair - 1, h)
+        for i in range(2):
+            gather(3, 2 * i, 0, HALF)
+            gather(3, 2 * i + 1, 0, HALF)
+            last_add(i, 0, nc.gpsimd)
+        for d in range(D):
+            gather(3, d, HALF, V)
+        for i in range(2):
+            last_add(i, 1, nc.vector)
         for h in range(2):
-            for j in (6, 7):
-                for d in range(D):
-                    gather(j, d, h * HALF, (h + 1) * HALF)
-                    add_up(j, d, h)
-            round_and_turn(3, h)
-            quantise_and_multiply(1, h, "vector" if h == 1 else "scalar")
+            quantise(0, h)
+        for h in (1, 0):
+            last_sum(h)
+        for h in (1, 0):
+            multiply(0, h)
+        for h in (1, 0):
+            quantise(1, h)
+            multiply(1, h)
+        for h in (1, 0):
             finish(h)

from contextlib import ExitStack

import concourse.mybir as mybir
from concourse.masks import make_identity

K, T, D, V, N = 1024, 2048, 4, 512, 256
FLOPS = 2 * K * V * N

F32 = mybir.dt.float32
BF16 = mybir.dt.bfloat16
I32 = mybir.dt.int32
U32 = mybir.dt.uint32
U16 = mybir.dt.uint16
U8 = mybir.dt.uint8
FP8X4 = mybir.dt.float8_e4m3fn_x4
ACT = mybir.ActivationFunctionType
ALU = mybir.AluOpType

P = 128
HALF = V // 2
CHUNK = 512
PACKERS = {1: "GVVV", 2: "SSSS", 3: "SSSS"}


def tile_picked_hash_lin_relu_sub_l_kernel(tc, xT, w_words, w_scales, b, offs, out):
    nc = tc.nc
    with ExitStack() as ctx:
        keep = ctx.enter_context(tc.tile_pool(name="keep", bufs=1))
        psum = ctx.enter_context(tc.psum_pool(name="psum", bufs=1))

        offsets = keep.tile([P, T // 16], U16, name="offsets")
        nc.sync.dma_start(offsets[:], offs)

        rows = xT.rearrange("(a p u e) n -> a u p e n", a=2, u=2, e=2)
        chunks = [slice(c, c + CHUNK) for c in range(0, T, CHUNK)]
        plane = [keep.tile([P, T], F32, name=f"plane{e}") for e in range(2)]
        for e in range(2):
            for cols in chunks:
                nc.sync.dma_start(out=plane[e][:, cols], in_=rows[0, 0][:, e, cols])
        raw = {}
        for pair in (1, 2, 3):
            for c, cols in enumerate(chunks):
                raw[(pair, c)] = keep.tile([P, 2, CHUNK], F32, name=f"raw{pair}_{c}", tag=f"raw{pair}_{c}")
                nc.sync.dma_start(out=raw[(pair, c)][:], in_=rows[pair // 2, pair % 2][:, :, cols])

        w_codes = keep.tile([P, 2, N], U32, name="w_codes", align_bytes=64)
        w_plane = keep.tile([P, 2, N], U8, name="w_plane", align_bytes=64)
        nc.vector.memset(w_plane[:].rearrange("p a n -> p (a n)").bitcast(U32), 0)
        for q in range(4):
            nc.sync.dma_start(
                out=w_plane[32 * q : 32 * q + 4, :, :].bitcast(I32),
                in_=w_scales[:, 4 * q : 4 * q + 4, :].rearrange("a r n -> r a n").bitcast(I32),
            )
        nc.sync.dma_start(
            out=w_codes[:].bitcast(I32),
            in_=w_words.rearrange("a p n r -> p a (n r)").bitcast(I32),
        )
        bias = [keep.tile([P, 1], F32, name=f"bias{m}") for m in range(2)]
        for m in range(2):
            nc.sync.dma_start(out=bias[m][:], in_=b[m * P : (m + 1) * P, :])

        ident = keep.tile([P, P], F32, name="ident")
        make_identity(nc, ident[:])

        widened = keep.tile([P, 4, V], F32, name="widened")
        nc.vector.memset(widened[:].rearrange("p s v -> p (s v)"), 0.0)
        warm = keep.tile([P, 1], F32, name="warm")
        nc.scalar.activation(out=warm[:], in_=widened[:, 0, 0:1], func=ACT.Relu)

        narrow = [keep.tile([P, T], BF16, name=f"narrow{e}", tag=f"narrow{e}") for e in range(2)]
        for cols in chunks:
            nc.vector.tensor_copy(out=narrow[0][:, cols], in_=plane[0][:, cols])
        for cols in chunks:
            nc.gpsimd.tensor_scalar(narrow[1][:, cols], plane[1][:, cols], 1.0, 0.0, ALU.mult, ALU.add)

        def piece(d, lo, hi):
            return offsets[:, (d * V + lo) // 16 : (d * V + hi) // 16]

        sums = {}
        count = {}

        def add_up(pair, h, e, src, total):
            if (pair, h) not in sums:
                sums[(pair, h)] = psum.tile([P, 2, 2, P], F32, name=f"sums{pair}_{h}", tag=f"sums{min(pair, 1)}_{h}")
                count[(pair, h)] = 0
            for vb in range(2):
                lo = h * HALF + vb * P
                nc.tensor.matmul(
                    sums[(pair, h)][:, vb, e, :],
                    lhsT=src[:, lo : lo + P],
                    rhs=ident[:],
                    start=(count[(pair, h)] == 0),
                    stop=(count[(pair, h)] == total - 1),
                    is_transpose=True,
                )
                count[(pair, h)] += 1

        picked = {(e, d): keep.tile([P, V], F32, name=f"picked{e}_{d}") for e in range(2) for d in (0, 2)}

        def first_pair(e, d, halves):
            for lo, hi in halves:
                if d % 2 == 0:
                    dst = picked[(e, d)][:]
                    nc.vector.tensor_copy(out=dst[:, lo:hi], in_=plane[e][:].indirect(piece(d, lo, hi)))
                else:
                    dst = widened[:, 2 * e + d // 2, :]
                    upper = dst.bitcast(BF16).rearrange("p (v h) -> p v h", h=2)
                    nc.scalar.activation(out=upper[:, lo:hi, 1], in_=narrow[e][:].indirect(piece(d, lo, hi)), func=ACT.Copy)
                for h in range(lo // HALF, hi // HALF):
                    add_up(0, h, e, dst, 4 * D)

        packed = {}
        last_chunk = len(chunks) - 1

        def pack(pair):
            tag = {1: "packed1", 2: "narrow1", 3: f"raw2_{last_chunk}"}[pair]
            packed[pair] = keep.tile([P, T], U32, name=f"packed{pair}", tag=tag)
            for c, (cols, who) in enumerate(zip(chunks, PACKERS[pair])):
                dst = packed[pair][:, cols].bitcast(BF16).rearrange("p (n e) -> p n e", e=2)
                src = raw[(pair, c)][:].rearrange("p e n -> p n e")
                if who == "G":
                    nc.gpsimd.tensor_scalar(dst, src, 1.0, 0.0, ALU.mult, ALU.add)
                elif who == "V":
                    nc.vector.tensor_copy(out=dst, in_=src)
                else:
                    nc.scalar.copy(out=dst, in_=src)

        words = {pair: keep.tile([P, D * V], U32, name=f"words{pair}") for pair in (1, 2, 3)}

        def looked_up(pair, d, lo, hi):
            return words[pair][:, d * V + lo : d * V + hi]

        def gather(pair, d, lo, hi):
            nc.vector.tensor_copy(out=looked_up(pair, d, lo, hi), in_=packed[pair][:].indirect(piece(d, lo, hi)))

        def middle_pair(pair):
            for i in range(2):
                gather(pair, 2 * i, 0, 2 * V)
                two = keep.tile([P, 2, V], F32, name=f"two{pair}_{i}")
                nc.gpsimd.tensor_tensor(
                    two[:],
                    looked_up(pair, 2 * i, 0, V).bitcast(BF16).rearrange("p (v e) -> p e v", e=2),
                    looked_up(pair, 2 * i + 1, 0, V).bitcast(BF16).rearrange("p (v e) -> p e v", e=2),
                    ALU.add,
                )
                for h in range(2):
                    for e in range(2):
                        add_up(pair, h, e, two[:, e, :], 8)

        back = {}
        rounded = {}

        def round_and_turn(pair, h):
            a, u = pair // 2, pair % 2
            group = pair // 2
            if group not in rounded:
                tag = f"raw3_{last_chunk}" if group == 0 else "rounded_last"
                rounded[group] = keep.tile([P, 2, 2, 2, P, 2], BF16, name=f"rounded{group}", tag=tag)
            dst = rounded[group][:, u, h]
            nc.scalar.copy(out=dst, in_=sums[(pair, h)][:].rearrange("v b e p -> v b p e"))
            turned = dst.rearrange("v b p e -> v (b p e)").bitcast(F32)
            if (a, h) not in back:
                back[(a, h)] = psum.tile([P, 2, HALF], F32, name=f"back{a}_{h}", tag=f"back{h}")
            for vb in range(2):
                nc.tensor.transpose(back[(a, h)][:, u, vb * P : (vb + 1) * P], turned[:, vb * P : (vb + 1) * P], ident[:])

        grouped = {
            (a, h): keep.tile([P, HALF * 4], BF16, name=f"grouped{a}_{h}", align_bytes=64) for a in range(2) for h in range(2)
        }

        def interleave(a, h):
            dst = grouped[(a, h)][:].bitcast(F32).rearrange("p (v u) -> p v u", u=2)
            if a == 0:
                nc.scalar.copy(out=dst, in_=back[(a, h)][:].rearrange("p u v -> p v u"))
            else:
                nc.scalar.copy(out=dst[:, :, 0], in_=back[(a, h)][:, 0, :])

        last_two = {}

        def last_add(i, h, engine):
            lo, hi = h * HALF, (h + 1) * HALF
            last_two[(i, h)] = keep.tile([P, 2 * HALF], F32, name=f"last_two{i}_{h}")
            engine.tensor_tensor(
                last_two[(i, h)][:],
                looked_up(3, 2 * i, lo, hi).bitcast(BF16),
                looked_up(3, 2 * i + 1, lo, hi).bitcast(BF16),
                ALU.add,
            )

        def last_sum(h):
            nc.vector.tensor_tensor(
                grouped[(1, h)][:].rearrange("p (v t) -> p v t", t=4)[:, :, 2:4],
                last_two[(0, h)][:].rearrange("p (v e) -> p v e", e=2),
                last_two[(1, h)][:].rearrange("p (v e) -> p v e", e=2),
                ALU.add,
            )

        codes = {}
        scales = {}

        def quantise(a, h):
            codes[(a, h)] = keep.tile([P, HALF], U32, name=f"codes{a}_{h}", align_bytes=64)
            scales[(a, h)] = keep.tile([P, HALF], U8, name=f"scales{a}_{h}", align_bytes=64)
            nc.vector.quantize_mx(out=codes[(a, h)][:].bitcast(FP8X4), scales=scales[(a, h)][:], in_=grouped[(a, h)][:])

        acc = {}

        def multiply(a, h):
            if a == 0 and h == 1:
                both = psum.tile([P, 2, HALF], F32, name="acc_second", tag="back1")
                acc[(0, 1)], acc[(1, 1)] = both[:, 0, :], both[:, 1, :]
            if a == 0 and h == 0:
                low = psum.tile([P, HALF], F32, name="acc_first0", tag="back0")
                high = psum.tile([P, HALF], F32, name="acc_first1", tag="sums1_1")
                acc[(0, 0)], acc[(1, 0)] = low[:], high[:]
            for m in range(2):
                nc.tensor.matmul_mx(
                    out=acc[(m, h)],
                    lhsT=w_codes[:, a, m * P : (m + 1) * P].bitcast(FP8X4),
                    lhsT_scale=w_plane[:, a, m * P : (m + 1) * P],
                    rhs=codes[(a, h)][:].bitcast(FP8X4),
                    rhs_scale=scales[(a, h)][:],
                    start=(a == 0 and (h == 0 or m == 0)),
                    stop=(a == 1 and (h == 0 or m == 1)),
                )

        def finish(h):
            for m in range(2):
                result = keep.tile([P, HALF], F32, name=f"result{m}_{h}")
                if m == 0 or h == 1:
                    nc.scalar.activation(out=result[:], in_=acc[(m, h)], func=ACT.Relu, bias=bias[m][:])
                else:
                    nc.vector.tensor_scalar(result[:], acc[(m, h)], bias[m][:], 0.0, ALU.add, ALU.max)
                nc.sync.dma_start(out=out[m * P : (m + 1) * P, h * HALF : (h + 1) * HALF], in_=result[:])

        whole = [(0, V)]
        halves = [(0, HALF), (HALF, V)]
        for e in range(2):
            for d in range(D):
                first_pair(e, d, halves if (e, d) == (1, D - 1) else whole)
        for pair in (1, 2, 3):
            pack(pair)
        for h in range(2):
            round_and_turn(0, h)
        for pair in (1, 2):
            middle_pair(pair)
            for h in range(2):
                round_and_turn(pair, h)
            for h in range(2):
                interleave(pair - 1, h)
        for i in range(2):
            gather(3, 2 * i, 0, HALF)
            gather(3, 2 * i + 1, 0, HALF)
            last_add(i, 0, nc.gpsimd)
        for d in range(D):
            gather(3, d, HALF, V)
        for i in range(2):
            last_add(i, 1, nc.vector)
        for h in range(2):
            quantise(0, h)
        for h in (1, 0):
            last_sum(h)
        for h in (1, 0):
            multiply(0, h)
        for h in (1, 0):
            quantise(1, h)
            multiply(1, h)
        for h in (1, 0):
            finish(h)
